import numpy as np
import ml_dtypes


def mxq(x, axis, fmt="e4m3"):
    dtype, down = {"e4m3": (ml_dtypes.float8_e4m3fn, 7), "e5m2": (ml_dtypes.float8_e5m2, 14)}[fmt]
    v = np.moveaxis(np.asarray(x, np.float32).astype(ml_dtypes.bfloat16).astype(np.float64), axis, -1)
    blocks = v.reshape(v.shape[:-1] + (-1, 32))
    amax = np.abs(blocks).max(-1, keepdims=True)
    byte = np.maximum(np.where(amax > 0, np.frexp(amax)[1] - 1 + 127, 0) - down, 1)
    scale = np.exp2(byte - 127.0)
    codes = (blocks / scale).astype(np.float32).astype(dtype).astype(np.float64)
    return np.moveaxis((codes * scale).reshape(v.shape), -1, axis)


WIDE = False


def mx_kscale(k):
    if not WIDE:
        return np.ones(k)
    levels = np.array([30, -30])
    if k % 512:
        return np.exp2(np.random.permutation(np.resize(levels, k // 32))).repeat(32)
    a = np.empty((k // 512, 16))
    for p in range(k // 512):
        a[p, :8] = np.random.permutation(np.resize(levels, 8))
        for g in range(8):
            far = levels[np.abs(levels - a[p, g]) >= 10]
            a[p, g + 8] = far[np.random.randint(len(far))]
    return np.exp2(a.ravel()).repeat(32)


def f64(x):
    return np.asarray(x).astype(np.float64)


def striped(idx):
    return np.tile(np.asarray(idx).reshape(-1, 16).T, (8, 1)).astype(np.uint16)


def unstriped(offs):
    return offs[:16].T.reshape(-1).astype(np.int64)


E2M1 = np.array([0.0, 0.5, 1.0, 1.5, 2.0, 3.0, 4.0, 6.0, -0.0, -0.5, -1.0, -1.5, -2.0, -3.0, -4.0, -6.0])


def pack_weight(w, fmt):
    k, n = w.shape
    w = f64(np.asarray(w, np.float32).astype(ml_dtypes.bfloat16)).reshape(k // 32, 32, n)
    amax = np.abs(w).max(1)
    if fmt in ("e4m3", "e5m2"):
        byte = np.frexp(amax)[1] - 1 + 127 - (7 if fmt == "e4m3" else 14)
    else:
        mant, ex = np.frexp(amax / 6.0)
        byte = np.where(mant > 0.5, ex, ex - 1) + 127
    byte = np.clip(np.where(amax > 0, byte, 1), 1, 254)
    scaled = (w * np.exp2(127.0 - byte)[:, None, :]).reshape(k, n).astype(np.float32)
    by_word = np.ascontiguousarray(scaled.reshape(k // 512, 128, 4, n).transpose(0, 1, 3, 2))
    if fmt in ("e4m3", "e5m2"):
        words = by_word.astype(ml_dtypes.float8_e4m3fn if fmt == "e4m3" else ml_dtypes.float8_e5m2).view(np.uint8)
    else:
        c = by_word.astype(ml_dtypes.float4_e2m1fn).view(np.uint8) & 0xF
        words = (c[..., 0::2] | (c[..., 1::2] << 4)).reshape(k // 512, 128, 2 * n)
    return np.ascontiguousarray(words), np.ascontiguousarray(byte.astype(np.uint8).reshape(k // 512, 16, n))


def unpack_weight(words, scales, fmt):
    g, _, n = scales.shape
    words = np.ascontiguousarray(words).reshape(g, 128, n, -1)
    if fmt in ("e4m3", "e5m2"):
        vals = words.view(ml_dtypes.float8_e4m3fn if fmt == "e4m3" else ml_dtypes.float8_e5m2).astype(np.float64)
    else:
        nib = np.empty((g, 128, n, 4), np.uint8)
        nib[..., 0::2] = words & 0xF
        nib[..., 1::2] = words >> 4
        vals = E2M1[nib]
    vals = vals * np.repeat(np.exp2(scales.astype(np.float64) - 127.0), 8, axis=1)[..., None]
    return vals.transpose(0, 1, 3, 2).reshape(g * 512, n)


K, T, J, I, R, Q = 512, 512, 256, 256, 512, 1024


def setup_inputs():
    n = np.random.standard_normal
    idx = np.random.permutation(T)[:J]
    idx2 = np.random.permutation(T)[:I]
    idx3 = np.random.permutation(Q)[:I]
    fk = mx_kscale(K)
    fr = mx_kscale(R)
    xtp = pack_weight(n((K, T)) / fk[:, None], "e5m2")
    wap = pack_weight(n((K, R)) * 0.5 / np.sqrt(K) * fk[:, None] * fr, "e2m1")
    wbp = pack_weight(n((K, R)) * 1 / np.sqrt(K) * fk[:, None] / fr, "e2m1")
    return {
        "xt_words": xtp[0],
        "xt_scales": xtp[1],
        "wa_words": wap[0],
        "wa_scales": wap[1],
        "oa": (n((R, J)) * 0.5 * fr[:, None]).astype(np.float32),
        "wb_words": wbp[0],
        "wb_scales": wbp[1],
        "old": (10.0 * n((J, Q))).astype(np.float32),
        "offs": striped(idx),
        "offs2": striped(idx2),
        "offs3": striped(idx3),
    }


def reference(xt_words, xt_scales, wa_words, wa_scales, oa, wb_words, wb_scales, old, offs, offs2, offs3):
    idx = unstriped(offs)
    idx2 = unstriped(offs2)
    idx3 = unstriped(offs3)
    xtu = unpack_weight(xt_words, xt_scales, "e5m2")
    wau = unpack_weight(wa_words, wa_scales, "e2m1")
    wbu = unpack_weight(wb_words, wb_scales, "e2m1")
    xtidxg = xtu[:, idx]
    za = wau.T @ xtidxg
    ha = np.maximum(za, f64(oa))
    xtidx2g = xtu[:, idx2]
    zb = wbu.T @ xtidx2g
    yb1 = np.pad(zb, ((0, 0), (1, 0)))[:, :I]
    hb = zb - 0.6 * yb1
    haq = mxq(ha, 0, "e5m2")
    hbq = mxq(hb, 0, "e5m2")
    a0 = haq.T @ hbq
    pp = np.zeros((J, Q))
    pp[:, idx3] = a0
    y = 0.04 * (pp - f64(old))
    return y

@@ -1,0 +1,202 @@
+from contextlib import ExitStack
+
+import concourse.mybir as mybir
+
+K, T, J, I, R, Q = 512, 512, 256, 256, 512, 1024
+FLOPS = 2 * K * R * J + 2 * K * R * I + 2 * R * J * I
+
+F32 = mybir.dt.float32
+BF16 = mybir.dt.bfloat16
+I32 = mybir.dt.int32
+U32 = mybir.dt.uint32
+U16 = mybir.dt.uint16
+U8 = mybir.dt.uint8
+E5M2X4 = mybir.dt.float8_e5m2_x4
+E2M1X4 = mybir.dt.float4_e2m1fn_x4
+MULT = mybir.AluOpType.mult
+ADD = mybir.AluOpType.add
+MAX = mybir.AluOpType.max
+COPY = mybir.ActivationFunctionType.Copy
+
+P = 128
+PACK = 4
+HALF = 128
+LAG = 0.6
+GAIN = 0.04
+
+
+def load_scale_plane(queue_low, queue_high, plane, scales):
+    rows = scales[0].bitcast(I32)
+    words = rows.shape[1]
+    queue_low.dma_start(out=plane[0:98, :].bitcast(I32), in_=rows[0:14, :].unsqueeze(0).to_broadcast([7, 14, words]))
+    queue_high.dma_start(out=plane[98:P, :].bitcast(I32), in_=rows[14:16, :].unsqueeze(0).to_broadcast([15, 2, words]))
+
+
+def deal_words(nc, dealt, raw):
+    nc.scalar.copy(
+        out=dealt[:].bitcast(U32).rearrange("p (t g) -> p t g", t=PACK),
+        in_=raw[:].bitcast(U32).rearrange("p (g t) -> p t g", t=PACK),
+    )
+
+
+def deal_scales(nc, dealt, raw):
+    nc.scalar.copy(
+        out=dealt[:].bitcast(U16).rearrange("p (t g) -> p t g", t=PACK),
+        in_=raw[:].bitcast(U16).rearrange("p (g t) -> p t g", t=PACK),
+    )
+
+
+def first_product(nc, bank, w_words, w_scales, x_words, x_scales, half):
+    cols = slice(half * HALF, (half + 1) * HALF)
+    for t in range(PACK):
+        nc.tensor.matmul_mx(
+            out=bank[:, t, :],
+            lhsT=w_words[:, 2 * P * t : 2 * P * (t + 1)].bitcast(E2M1X4),
+            lhsT_scale=w_scales[:, P * t : P * (t + 1)],
+            rhs=x_words[:, cols].bitcast(E5M2X4),
+            rhs_scale=x_scales[:, cols],
+            start=True,
+            stop=True,
+        )
+
+
+def tile_list_meet_added_lagged_placed_kernel(
+    tc, xt_words, xt_scales, wa_words, wa_scales, oa, wb_words, wb_scales, old, offs, offs2, offs3, out
+):
+    nc = tc.nc
+    with ExitStack() as ctx:
+        lists = ctx.enter_context(tc.tile_pool(name="lists", bufs=1))
+        sb = ctx.enter_context(tc.tile_pool(name="sb", bufs=1))
+        psum = ctx.enter_context(tc.psum_pool(name="psum", bufs=1))
+
+        list_a = lists.tile([P, J // 16], U16, name="list_a")
+        list_b = lists.tile([P, I // 16], U16, name="list_b")
+        list_q = lists.tile([P, I // 16], U16, name="list_q")
+
+        x_words = sb.tile([P, T], U32, name="x_words", align_bytes=64)
+        x_scales = sb.tile([P, T], U8, name="x_scales", align_bytes=64)
+        wa_raw = sb.tile([P, 2 * R], U8, name="wa_raw", align_bytes=64)
+        wb_raw = sb.tile([P, 2 * R], U8, name="wb_raw", align_bytes=64)
+        wa_scales_raw = sb.tile([P, R], U8, name="wa_scales_raw", align_bytes=64)
+        wb_scales_raw = sb.tile([P, R], U8, name="wb_scales_raw", align_bytes=64)
+        oa_slots = sb.tile([P, PACK, J], F32, name="oa_slots", align_bytes=64)
+        old_rows = [sb.tile([P, Q], F32, name=f"old_rows{h}", align_bytes=64) for h in range(2)]
+
+        nc.sync.dma_start(list_b[:], offs2)
+        nc.sync.dma_start(out=x_words[:].bitcast(I32), in_=xt_words[0].rearrange("p c r -> p (c r)").bitcast(I32))
+        nc.scalar.dma_start(out=wb_raw[:].bitcast(I32), in_=wb_words[0].bitcast(I32))
+        nc.sync.dma_start(list_a[:], offs)
+        load_scale_plane(nc.scalar, nc.sync, x_scales, xt_scales)
+        load_scale_plane(nc.scalar, nc.sync, wb_scales_raw, wb_scales)
+        load_scale_plane(nc.sync, nc.sync, wa_scales_raw, wa_scales)
+        nc.sync.dma_start(out=wa_raw[:].bitcast(I32), in_=wa_words[0].bitcast(I32))
+        oa_by_parity = oa.rearrange("(g t u) j -> u g t j", t=PACK, u=2)
+        for u in range(2):
+            nc.sync.dma_start(out=oa_slots[u:P:2, :, :], in_=oa_by_parity[u])
+        nc.sync.dma_start(list_q[:], offs3)
+        for h in range(2):
+            nc.sync.dma_start(out=old_rows[h][:], in_=old[h * P : (h + 1) * P, :])
+
+        boards = [sb.tile([P, Q], F32, name=f"board{h}", align_bytes=64) for h in range(2)]
+        lagged = sb.tile([P, I, PACK], F32, name="lagged", align_bytes=64)
+        nc.vector.memset(lagged[:, 0, :], 0.0)
+        for h in range(2):
+            nc.vector.memset(boards[h][:], 0.0)
+
+        xb_words = sb.tile([P, I], U32, name="xb_words", align_bytes=64)
+        xb_scales = sb.tile([P, I], U8, name="xb_scales", align_bytes=64)
+        xa_words = sb.tile([P, J], U32, name="xa_words", align_bytes=64)
+        xa_scales = sb.tile([P, J], U8, name="xa_scales", align_bytes=64)
+        nc.vector.tensor_copy(xb_words[:], x_words[:].indirect(list_b[:]))
+        nc.vector.tensor_copy(xb_scales[:], x_scales[:].indirect(list_b[:]))
+        nc.vector.tensor_copy(xa_words[:], x_words[:].indirect(list_a[:]))
+        nc.vector.tensor_copy(xa_scales[:], x_scales[:].indirect(list_a[:]))
+
+        wa_dealt = sb.tile([P, 2 * R], U8, name="wa_dealt", align_bytes=64)
+        wb_dealt = sb.tile([P, 2 * R], U8, name="wb_dealt", align_bytes=64)
+        wa_scales_dealt = sb.tile([P, R], U8, name="wa_scales_dealt", align_bytes=64)
+        wb_scales_dealt = sb.tile([P, R], U8, name="wb_scales_dealt", align_bytes=64)
+        deal_words(nc, wb_dealt, wb_raw)
+        deal_scales(nc, wb_scales_dealt, wb_scales_raw)
+        deal_words(nc, wa_dealt, wa_raw)
+
+        zb = [psum.tile([P, PACK, HALF], F32, name=f"zb{h}") for h in range(2)]
+        za = [psum.tile([P, PACK, HALF], F32, name=f"za{h}") for h in range(2)]
+        scores = [psum.tile([P, I], F32, name=f"scores{h}") for h in range(2)]
+
+        for h in range(2):
+            first_product(nc, zb[h], wb_dealt, wb_scales_dealt, xb_words, xb_scales, h)
+        for h in range(2):
+            width = min(HALF, I - 1 - h * HALF)
+            nc.scalar.copy(
+                out=lagged[:, h * HALF + 1 : h * HALF + 1 + width, :],
+                in_=zb[h][:, :, 0:width].rearrange("p t i -> p i t"),
+            )
+        deal_scales(nc, wa_scales_dealt, wa_scales_raw)
+        for h in range(2):
+            first_product(nc, za[h], wa_dealt, wa_scales_dealt, xa_words, xa_scales, h)
+
+        oa_woven = [sb.tile([P, HALF, PACK], F32, name=f"oa_woven{h}", align_bytes=64) for h in range(2)]
+        for h in range(2):
+            nc.gpsimd.tensor_scalar(
+                oa_woven[h][:],
+                oa_slots[:, :, h * HALF : (h + 1) * HALF].rearrange("p t j -> p j t"),
+                1.0,
+                0.0,
+                MULT,
+                ADD,
+            )
+
+        hb = sb.tile([P, I, PACK], BF16, name="hb", align_bytes=64)
+        ha = [sb.tile([P, HALF, PACK], BF16, name=f"ha{h}", align_bytes=64) for h in range(2)]
+        hb_words = sb.tile([P, I], U32, name="hb_words", align_bytes=64)
+        hb_scales = sb.tile([P, I], U8, name="hb_scales", align_bytes=64)
+        ha_words = [sb.tile([P, HALF], U32, name=f"ha_words{h}", align_bytes=64) for h in range(2)]
+        ha_scales = [sb.tile([P, HALF], U8, name=f"ha_scales{h}", align_bytes=64) for h in range(2)]
+        staged = [sb.tile([P, I], F32, name=f"staged{h}", align_bytes=64) for h in range(2)]
+
+        for h in range(2):
+            cols = slice(h * HALF, (h + 1) * HALF)
+            nc.vector.scalar_tensor_tensor(
+                hb[:, cols, :], lagged[:, cols, :], -LAG, zb[h][:].rearrange("p t i -> p i t"), MULT, ADD
+            )
+
+        def raise_rows(h):
+            nc.vector.tensor_tensor(ha[h][:], za[h][:].rearrange("p t j -> p j t"), oa_woven[h][:], MAX)
+
+        def meet(h):
+            nc.vector.quantize_mx(
+                out=ha_words[h][:].bitcast(E5M2X4),
+                scales=ha_scales[h][:],
+                in_=ha[h][:].rearrange("p j t -> p (j t)"),
+            )
+            nc.tensor.matmul_mx(
+                out=scores[h][:],
+                lhsT=ha_words[h][:].bitcast(E5M2X4),
+                lhsT_scale=ha_scales[h][:],
+                rhs=hb_words[:].bitcast(E5M2X4),
+                rhs_scale=hb_scales[:],
+                start=True,
+                stop=True,
+            )
+            nc.scalar.activation(staged[h][:], scores[h][:], COPY, scale=GAIN)
+
+        raise_rows(0)
+        nc.vector.quantize_mx(
+            out=hb_words[:].bitcast(E5M2X4), scales=hb_scales[:], in_=hb[:].rearrange("p i t -> p (i t)")
+        )
+        meet(0)
+        split = I // 2
+        nc.scalar.activation(boards[0][:].indirect(list_q[:, 0 : split // 16]), staged[0][:, 0:split], COPY)
+        raise_rows(1)
+        meet(1)
+        nc.vector.tensor_copy(boards[0][:].indirect(list_q[:, split // 16 : I // 16]), staged[0][:, split:I])
+        nc.scalar.activation(boards[1][:].indirect(list_q[:]), staged[1][:], COPY)
+
+        pieces = [(0, 0, 512), (0, 512, 1024), (1, 0, 512), (1, 512, 768), (1, 768, 1024)]
+        for n, (h, lo, hi) in enumerate(pieces):
+            result = sb.tile([P, hi - lo], F32, name=f"result{n}", align_bytes=64)
+            nc.vector.scalar_tensor_tensor(
+                result[:], old_rows[h][:, lo:hi], -GAIN, boards[h][:, lo:hi], MULT, ADD
+            )
+            nc.sync.dma_start(out=out[h * P : (h + 1) * P, lo:hi], in_=result[:])

@@ -32,17 +32,10 @@ def load_scale_plane(queue_low, queue_high, plane, scales):
     queue_high.dma_start(out=plane[98:P, :].bitcast(I32), in_=rows[14:16, :].unsqueeze(0).to_broadcast([15, 2, words]))
 
 
-def deal_words(nc, dealt, raw):
-    nc.scalar.copy(
-        out=dealt[:].bitcast(U32).rearrange("p (t g) -> p t g", t=PACK),
-        in_=raw[:].bitcast(U32).rearrange("p (g t) -> p t g", t=PACK),
-    )
-
-
-def deal_scales(nc, dealt, raw):
-    nc.scalar.copy(
-        out=dealt[:].bitcast(U16).rearrange("p (t g) -> p t g", t=PACK),
-        in_=raw[:].bitcast(U16).rearrange("p (g t) -> p t g", t=PACK),
+def deal_columns(copy, word, dealt, raw):
+    copy(
+        out=dealt[:].bitcast(word).rearrange("p (t b w) -> p t b w", t=PACK, b=16),
+        in_=raw[:].bitcast(word).rearrange("p (b t w) -> p t b w", t=PACK, b=16),
     )
 
 
@@ -83,25 +76,31 @@ def tile_list_meet_added_lagged_placed_kernel(
         old_rows = [sb.tile([P, Q], F32, name=f"old_rows{h}", align_bytes=64) for h in range(2)]
 
         nc.sync.dma_start(list_b[:], offs2)
-        nc.sync.dma_start(out=x_words[:].bitcast(I32), in_=xt_words[0].rearrange("p c r -> p (c r)").bitcast(I32))
         nc.scalar.dma_start(out=wb_raw[:].bitcast(I32), in_=wb_words[0].bitcast(I32))
-        nc.sync.dma_start(list_a[:], offs)
-        load_scale_plane(nc.scalar, nc.sync, x_scales, xt_scales)
-        load_scale_plane(nc.scalar, nc.sync, wb_scales_raw, wb_scales)
-        load_scale_plane(nc.sync, nc.sync, wa_scales_raw, wa_scales)
+        nc.sync.dma_start(out=x_words[:].bitcast(I32), in_=xt_words[0].rearrange("p c r -> p (c r)").bitcast(I32))
+        load_scale_plane(nc.sync, nc.scalar, x_scales, xt_scales)
+        load_scale_plane(nc.sync, nc.scalar, wb_scales_raw, wb_scales)
+        load_scale_plane(nc.gpsimd, nc.gpsimd, wa_scales_raw, wa_scales)
         nc.sync.dma_start(out=wa_raw[:].bitcast(I32), in_=wa_words[0].bitcast(I32))
-        oa_by_parity = oa.rearrange("(g t u) j -> u g t j", t=PACK, u=2)
-        for u in range(2):
-            nc.sync.dma_start(out=oa_slots[u:P:2, :, :], in_=oa_by_parity[u])
+        nc.sync.dma_start(list_a[:], offs)
+        oa_by_slot = oa.rearrange("(b t u) j -> t b u j", t=PACK, u=8)
+        for t in range(PACK):
+            nc.sync.dma_start(out=oa_slots[:, t, :], in_=oa_by_slot[t])
         nc.sync.dma_start(list_q[:], offs3)
         for h in range(2):
             nc.sync.dma_start(out=old_rows[h][:], in_=old[h * P : (h + 1) * P, :])
 
         boards = [sb.tile([P, Q], F32, name=f"board{h}", align_bytes=64) for h in range(2)]
         lagged = sb.tile([P, I, PACK], F32, name="lagged", align_bytes=64)
-        nc.vector.memset(lagged[:, 0, :], 0.0)
         for h in range(2):
             nc.vector.memset(boards[h][:], 0.0)
+        nc.scalar.copy(out=lagged[:, 0, :], in_=boards[0][:, 0:PACK])
+
+        wa_dealt = sb.tile([P, 2 * R], U8, name="wa_dealt", align_bytes=64)
+        wb_dealt = sb.tile([P, 2 * R], U8, name="wb_dealt", align_bytes=64)
+        wa_scales_dealt = sb.tile([P, R], U8, name="wa_scales_dealt", align_bytes=64)
+        wb_scales_dealt = sb.tile([P, R], U8, name="wb_scales_dealt", align_bytes=64)
+        deal_columns(nc.vector.tensor_copy, I32, wb_dealt, wb_raw)
 
         xb_words = sb.tile([P, I], U32, name="xb_words", align_bytes=64)
         xb_scales = sb.tile([P, I], U8, name="xb_scales", align_bytes=64)
@@ -112,13 +111,9 @@ def tile_list_meet_added_lagged_placed_kernel(
         nc.vector.tensor_copy(xa_words[:], x_words[:].indirect(list_a[:]))
         nc.vector.tensor_copy(xa_scales[:], x_scales[:].indirect(list_a[:]))
 
-        wa_dealt = sb.tile([P, 2 * R], U8, name="wa_dealt", align_bytes=64)
-        wb_dealt = sb.tile([P, 2 * R], U8, name="wb_dealt", align_bytes=64)
-        wa_scales_dealt = sb.tile([P, R], U8, name="wa_scales_dealt", align_bytes=64)
-        wb_scales_dealt = sb.tile([P, R], U8, name="wb_scales_dealt", align_bytes=64)
-        deal_words(nc, wb_dealt, wb_raw)
-        deal_scales(nc, wb_scales_dealt, wb_scales_raw)
-        deal_words(nc, wa_dealt, wa_raw)
+        deal_columns(nc.scalar.copy, U32, wb_scales_dealt, wb_scales_raw)
+        deal_columns(nc.gpsimd.tensor_copy, U32, wa_dealt, wa_raw)
+        deal_columns(nc.gpsimd.tensor_copy, U32, wa_scales_dealt, wa_scales_raw)
 
         zb = [psum.tile([P, PACK, HALF], F32, name=f"zb{h}") for h in range(2)]
         za = [psum.tile([P, PACK, HALF], F32, name=f"za{h}") for h in range(2)]
@@ -132,7 +127,6 @@ def tile_list_meet_added_lagged_placed_kernel(
                 out=lagged[:, h * HALF + 1 : h * HALF + 1 + width, :],
                 in_=zb[h][:, :, 0:width].rearrange("p t i -> p i t"),
             )
-        deal_scales(nc, wa_scales_dealt, wa_scales_raw)
         for h in range(2):
             first_product(nc, za[h], wa_dealt, wa_scales_dealt, xa_words, xa_scales, h)
 
@@ -148,7 +142,8 @@ def tile_list_meet_added_lagged_placed_kernel(
             )
 
         hb = sb.tile([P, I, PACK], BF16, name="hb", align_bytes=64)
-        ha = [sb.tile([P, HALF, PACK], BF16, name=f"ha{h}", align_bytes=64) for h in range(2)]
+        ha_first = sb.tile([P, HALF, PACK], BF16, name="ha_first", align_bytes=64)
+        ha = [ha_first[:], hb[:, 0:HALF, :]]
         hb_words = sb.tile([P, I], U32, name="hb_words", align_bytes=64)
         hb_scales = sb.tile([P, I], U8, name="hb_scales", align_bytes=64)
         ha_words = [sb.tile([P, HALF], U32, name=f"ha_words{h}", align_bytes=64) for h in range(2)]
@@ -162,13 +157,13 @@ def tile_list_meet_added_lagged_placed_kernel(
             )
 
         def raise_rows(h):
-            nc.vector.tensor_tensor(ha[h][:], za[h][:].rearrange("p t j -> p j t"), oa_woven[h][:], MAX)
+            nc.vector.tensor_tensor(ha[h], za[h][:].rearrange("p t j -> p j t"), oa_woven[h][:], MAX)
 
         def meet(h):
             nc.vector.quantize_mx(
                 out=ha_words[h][:].bitcast(E5M2X4),
                 scales=ha_scales[h][:],
-                in_=ha[h][:].rearrange("p j t -> p (j t)"),
+                in_=ha[h].rearrange("p j t -> p (j t)"),
             )
             nc.tensor.matmul_mx(
                 out=scores[h][:],
@@ -186,14 +181,12 @@ def tile_list_meet_added_lagged_placed_kernel(
             out=hb_words[:].bitcast(E5M2X4), scales=hb_scales[:], in_=hb[:].rearrange("p i t -> p (i t)")
         )
         meet(0)
-        split = I // 2
-        nc.scalar.activation(boards[0][:].indirect(list_q[:, 0 : split // 16]), staged[0][:, 0:split], COPY)
         raise_rows(1)
         meet(1)
-        nc.vector.tensor_copy(boards[0][:].indirect(list_q[:, split // 16 : I // 16]), staged[0][:, split:I])
+        nc.vector.tensor_copy(boards[0][:].indirect(list_q[:]), staged[0][:])
         nc.scalar.activation(boards[1][:].indirect(list_q[:]), staged[1][:], COPY)
 
-        pieces = [(0, 0, 512), (0, 512, 1024), (1, 0, 512), (1, 512, 768), (1, 768, 1024)]
+        pieces = [(0, 0, 256), (0, 256, 512), (0, 512, 1024), (1, 0, 512), (1, 512, 768), (1, 768, 1024)]
         for n, (h, lo, hi) in enumerate(pieces):
             result = sb.tile([P, hi - lo], F32, name=f"result{n}", align_bytes=64)
             nc.vector.scalar_tensor_tensor(

@@ -32,6 +32,14 @@ def load_scale_plane(queue_low, queue_high, plane, scales):
     queue_high.dma_start(out=plane[98:P, :].bitcast(I32), in_=rows[14:16, :].unsqueeze(0).to_broadcast([15, 2, words]))
 
 
+def load_scale_quadrant(queue, plane, scales, quad):
+    rows = scales[0].bitcast(I32)[4 * quad : 4 * quad + 4, :]
+    queue.dma_start(
+        out=plane[32 * quad : 32 * quad + 32, :].bitcast(I32),
+        in_=rows.unsqueeze(0).to_broadcast([8, 4, rows.shape[1]]),
+    )
+
+
 def deal_columns(copy, word, dealt, raw):
     copy(
         out=dealt[:].bitcast(word).rearrange("p (t b w) -> p t b w", t=PACK, b=16),
@@ -72,7 +80,8 @@ def tile_list_meet_added_lagged_placed_kernel(
         wb_raw = sb.tile([P, 2 * R], U8, name="wb_raw", align_bytes=64)
         wa_scales_raw = sb.tile([P, R], U8, name="wa_scales_raw", align_bytes=64)
         wb_scales_raw = sb.tile([P, R], U8, name="wb_scales_raw", align_bytes=64)
-        oa_slots = sb.tile([P, PACK, J], F32, name="oa_slots", align_bytes=64)
+        shared = sb.tile([P, 384 + PACK * J], F32, name="shared", align_bytes=64)
+        oa_slots = shared[:, 384:].rearrange("p (t j) -> p t j", t=PACK)
         old_rows = [sb.tile([P, Q], F32, name=f"old_rows{h}", align_bytes=64) for h in range(2)]
 
         nc.sync.dma_start(list_b[:], offs2)
@@ -80,9 +89,10 @@ def tile_list_meet_added_lagged_placed_kernel(
         nc.sync.dma_start(out=x_words[:].bitcast(I32), in_=xt_words[0].rearrange("p c r -> p (c r)").bitcast(I32))
         load_scale_plane(nc.sync, nc.scalar, x_scales, xt_scales)
         load_scale_plane(nc.sync, nc.scalar, wb_scales_raw, wb_scales)
-        load_scale_plane(nc.gpsimd, nc.gpsimd, wa_scales_raw, wa_scales)
-        nc.sync.dma_start(out=wa_raw[:].bitcast(I32), in_=wa_words[0].bitcast(I32))
+        nc.gpsimd.dma_start(out=wa_raw[:].bitcast(I32), in_=wa_words[0].bitcast(I32))
         nc.sync.dma_start(list_a[:], offs)
+        for quad in range(4):
+            load_scale_quadrant(nc.sync, wa_scales_raw, wa_scales, quad)
         oa_by_slot = oa.rearrange("(b t u) j -> t b u j", t=PACK, u=8)
         for t in range(PACK):
             nc.sync.dma_start(out=oa_slots[:, t, :], in_=oa_by_slot[t])
@@ -112,7 +122,7 @@ def tile_list_meet_added_lagged_placed_kernel(
         nc.vector.tensor_copy(xa_scales[:], x_scales[:].indirect(list_a[:]))
 
         deal_columns(nc.scalar.copy, U32, wb_scales_dealt, wb_scales_raw)
-        deal_columns(nc.gpsimd.tensor_copy, U32, wa_dealt, wa_raw)
+        deal_columns(nc.scalar.copy, U32, wa_dealt, wa_raw)
         deal_columns(nc.gpsimd.tensor_copy, U32, wa_scales_dealt, wa_scales_raw)
 
         zb = [psum.tile([P, PACK, HALF], F32, name=f"zb{h}") for h in range(2)]
@@ -121,50 +131,39 @@ def tile_list_meet_added_lagged_placed_kernel(
 
         for h in range(2):
             first_product(nc, zb[h], wb_dealt, wb_scales_dealt, xb_words, xb_scales, h)
-        for h in range(2):
             width = min(HALF, I - 1 - h * HALF)
             nc.scalar.copy(
                 out=lagged[:, h * HALF + 1 : h * HALF + 1 + width, :],
                 in_=zb[h][:, :, 0:width].rearrange("p t i -> p i t"),
             )
-        for h in range(2):
             first_product(nc, za[h], wa_dealt, wa_scales_dealt, xa_words, xa_scales, h)
 
-        oa_woven = [sb.tile([P, HALF, PACK], F32, name=f"oa_woven{h}", align_bytes=64) for h in range(2)]
-        for h in range(2):
-            nc.gpsimd.tensor_scalar(
-                oa_woven[h][:],
-                oa_slots[:, :, h * HALF : (h + 1) * HALF].rearrange("p t j -> p j t"),
-                1.0,
-                0.0,
-                MULT,
-                ADD,
-            )
-
-        hb = sb.tile([P, I, PACK], BF16, name="hb", align_bytes=64)
-        ha_first = sb.tile([P, HALF, PACK], BF16, name="ha_first", align_bytes=64)
-        ha = [ha_first[:], hb[:, 0:HALF, :]]
+        hb = shared[:, 0:512].bitcast(BF16).rearrange("p (i t) -> p i t", t=PACK)
+        ha = sb.tile([P, HALF, PACK], BF16, name="ha", align_bytes=64)
         hb_words = sb.tile([P, I], U32, name="hb_words", align_bytes=64)
         hb_scales = sb.tile([P, I], U8, name="hb_scales", align_bytes=64)
         ha_words = [sb.tile([P, HALF], U32, name=f"ha_words{h}", align_bytes=64) for h in range(2)]
         ha_scales = [sb.tile([P, HALF], U8, name=f"ha_scales{h}", align_bytes=64) for h in range(2)]
         staged = [sb.tile([P, I], F32, name=f"staged{h}", align_bytes=64) for h in range(2)]
 
-        for h in range(2):
+        def lag_columns(h):
             cols = slice(h * HALF, (h + 1) * HALF)
             nc.vector.scalar_tensor_tensor(
                 hb[:, cols, :], lagged[:, cols, :], -LAG, zb[h][:].rearrange("p t i -> p i t"), MULT, ADD
             )
 
         def raise_rows(h):
-            nc.vector.tensor_tensor(ha[h], za[h][:].rearrange("p t j -> p j t"), oa_woven[h][:], MAX)
+            own = oa_slots[:, :, h * HALF : (h + 1) * HALF]
+            nc.vector.tensor_tensor(ha[:], za[h][:].rearrange("p t j -> p j t"), own.rearrange("p t j -> p j t"), MAX)
 
-        def meet(h):
+        def quantize_rows(h):
             nc.vector.quantize_mx(
                 out=ha_words[h][:].bitcast(E5M2X4),
                 scales=ha_scales[h][:],
-                in_=ha[h].rearrange("p j t -> p (j t)"),
+                in_=ha[:].rearrange("p j t -> p (j t)"),
             )
+
+        def meet(h):
             nc.tensor.matmul_mx(
                 out=scores[h][:],
                 lhsT=ha_words[h][:].bitcast(E5M2X4),
@@ -176,17 +175,21 @@ def tile_list_meet_added_lagged_placed_kernel(
             )
             nc.scalar.activation(staged[h][:], scores[h][:], COPY, scale=GAIN)
 
+        lag_columns(0)
         raise_rows(0)
+        lag_columns(1)
+        quantize_rows(0)
         nc.vector.quantize_mx(
-            out=hb_words[:].bitcast(E5M2X4), scales=hb_scales[:], in_=hb[:].rearrange("p i t -> p (i t)")
+            out=hb_words[:].bitcast(E5M2X4), scales=hb_scales[:], in_=shared[:, 0:512].bitcast(BF16)
         )
         meet(0)
         raise_rows(1)
+        quantize_rows(1)
         meet(1)
         nc.vector.tensor_copy(boards[0][:].indirect(list_q[:]), staged[0][:])
         nc.scalar.activation(boards[1][:].indirect(list_q[:]), staged[1][:], COPY)
 
-        pieces = [(0, 0, 256), (0, 256, 512), (0, 512, 1024), (1, 0, 512), (1, 512, 768), (1, 768, 1024)]
+        pieces = [(h, lo, lo + 256) for h in range(2) for lo in range(0, Q, 256)]
         for n, (h, lo, hi) in enumerate(pieces):
             result = sb.tile([P, hi - lo], F32, name=f"result{n}", align_bytes=64)
             nc.vector.scalar_tensor_tensor(

@@ -80,49 +80,55 @@ def tile_list_meet_added_lagged_placed_kernel(
         wb_raw = sb.tile([P, 2 * R], U8, name="wb_raw", align_bytes=64)
         wa_scales_raw = sb.tile([P, R], U8, name="wa_scales_raw", align_bytes=64)
         wb_scales_raw = sb.tile([P, R], U8, name="wb_scales_raw", align_bytes=64)
-        shared = sb.tile([P, 384 + PACK * J], F32, name="shared", align_bytes=64)
-        oa_slots = shared[:, 384:].rearrange("p (t j) -> p t j", t=PACK)
+        oa_first = sb.tile([P, PACK, HALF], F32, name="oa_first", tag="reused", align_bytes=64)
+        oa_second = sb.tile([P, PACK, HALF], F32, name="oa_second", tag="reused_second", align_bytes=64)
+        oa_slots = [oa_first, oa_second]
         old_rows = [sb.tile([P, Q], F32, name=f"old_rows{h}", align_bytes=64) for h in range(2)]
 
         nc.sync.dma_start(list_b[:], offs2)
-        nc.scalar.dma_start(out=wb_raw[:].bitcast(I32), in_=wb_words[0].bitcast(I32))
         nc.sync.dma_start(out=x_words[:].bitcast(I32), in_=xt_words[0].rearrange("p c r -> p (c r)").bitcast(I32))
-        load_scale_plane(nc.sync, nc.scalar, x_scales, xt_scales)
-        load_scale_plane(nc.sync, nc.scalar, wb_scales_raw, wb_scales)
+        for quad in range(4):
+            load_scale_quadrant(nc.sync, x_scales, xt_scales, quad)
+        nc.sync.dma_start(out=wb_raw[:].bitcast(I32), in_=wb_words[0].bitcast(I32))
+        load_scale_plane(nc.scalar, nc.gpsimd, wb_scales_raw, wb_scales)
         nc.gpsimd.dma_start(out=wa_raw[:].bitcast(I32), in_=wa_words[0].bitcast(I32))
         nc.sync.dma_start(list_a[:], offs)
         for quad in range(4):
             load_scale_quadrant(nc.sync, wa_scales_raw, wa_scales, quad)
         oa_by_slot = oa.rearrange("(b t u) j -> t b u j", t=PACK, u=8)
-        for t in range(PACK):
-            nc.sync.dma_start(out=oa_slots[:, t, :], in_=oa_by_slot[t])
+        for h in range(2):
+            for t in range(PACK):
+                nc.sync.dma_start(out=oa_slots[h][:, t, :], in_=oa_by_slot[t][:, :, h * HALF : (h + 1) * HALF])
         nc.sync.dma_start(list_q[:], offs3)
         for h in range(2):
             nc.sync.dma_start(out=old_rows[h][:], in_=old[h * P : (h + 1) * P, :])
 
         boards = [sb.tile([P, Q], F32, name=f"board{h}", align_bytes=64) for h in range(2)]
         lagged = sb.tile([P, I, PACK], F32, name="lagged", align_bytes=64)
-        for h in range(2):
-            nc.vector.memset(boards[h][:], 0.0)
+        nc.vector.memset(boards[0][:, 0:511], 0.0)
+        nc.vector.memset(boards[0][:, 511:Q], 0.0)
+        nc.vector.memset(boards[1][:], 0.0)
         nc.scalar.copy(out=lagged[:, 0, :], in_=boards[0][:, 0:PACK])
 
         wa_dealt = sb.tile([P, 2 * R], U8, name="wa_dealt", align_bytes=64)
         wb_dealt = sb.tile([P, 2 * R], U8, name="wb_dealt", align_bytes=64)
         wa_scales_dealt = sb.tile([P, R], U8, name="wa_scales_dealt", align_bytes=64)
         wb_scales_dealt = sb.tile([P, R], U8, name="wb_scales_dealt", align_bytes=64)
-        deal_columns(nc.vector.tensor_copy, I32, wb_dealt, wb_raw)
+        deal_columns(nc.scalar.copy, U32, wb_dealt, wb_raw)
 
         xb_words = sb.tile([P, I], U32, name="xb_words", align_bytes=64)
         xb_scales = sb.tile([P, I], U8, name="xb_scales", align_bytes=64)
         xa_words = sb.tile([P, J], U32, name="xa_words", align_bytes=64)
         xa_scales = sb.tile([P, J], U8, name="xa_scales", align_bytes=64)
-        nc.vector.tensor_copy(xb_words[:], x_words[:].indirect(list_b[:]))
-        nc.vector.tensor_copy(xb_scales[:], x_scales[:].indirect(list_b[:]))
-        nc.vector.tensor_copy(xa_words[:], x_words[:].indirect(list_a[:]))
-        nc.vector.tensor_copy(xa_scales[:], x_scales[:].indirect(list_a[:]))
+        for words, scales, picks in ((xb_words, xb_scales, list_b), (xa_words, xa_scales, list_a)):
+            for h in range(2):
+                cols = slice(h * HALF, (h + 1) * HALF)
+                entries = picks[:, h * HALF // 16 : (h + 1) * HALF // 16]
+                nc.vector.tensor_copy(words[:, cols], x_words[:].indirect(entries))
+                nc.vector.tensor_copy(scales[:, cols], x_scales[:].indirect(entries))
 
         deal_columns(nc.scalar.copy, U32, wb_scales_dealt, wb_scales_raw)
-        deal_columns(nc.scalar.copy, U32, wa_dealt, wa_raw)
+        deal_columns(nc.gpsimd.tensor_copy, U32, wa_dealt, wa_raw)
         deal_columns(nc.gpsimd.tensor_copy, U32, wa_scales_dealt, wa_scales_raw)
 
         zb = [psum.tile([P, PACK, HALF], F32, name=f"zb{h}") for h in range(2)]
@@ -136,15 +142,15 @@ def tile_list_meet_added_lagged_placed_kernel(
                 out=lagged[:, h * HALF + 1 : h * HALF + 1 + width, :],
                 in_=zb[h][:, :, 0:width].rearrange("p t i -> p i t"),
             )
+        for h in range(2):
             first_product(nc, za[h], wa_dealt, wa_scales_dealt, xa_words, xa_scales, h)
 
-        hb = shared[:, 0:512].bitcast(BF16).rearrange("p (i t) -> p i t", t=PACK)
-        ha = sb.tile([P, HALF, PACK], BF16, name="ha", align_bytes=64)
-        hb_words = sb.tile([P, I], U32, name="hb_words", align_bytes=64)
+        hb = sb.tile([P, I, PACK], BF16, name="hb", align_bytes=64)
+        ha_first = sb.tile([P, HALF, PACK], BF16, name="ha_first", align_bytes=64)
+        ha = [ha_first[:], hb[:, 0:HALF, :]]
         hb_scales = sb.tile([P, I], U8, name="hb_scales", align_bytes=64)
         ha_words = [sb.tile([P, HALF], U32, name=f"ha_words{h}", align_bytes=64) for h in range(2)]
         ha_scales = [sb.tile([P, HALF], U8, name=f"ha_scales{h}", align_bytes=64) for h in range(2)]
-        staged = [sb.tile([P, I], F32, name=f"staged{h}", align_bytes=64) for h in range(2)]
 
         def lag_columns(h):
             cols = slice(h * HALF, (h + 1) * HALF)
@@ -153,14 +159,14 @@ def tile_list_meet_added_lagged_placed_kernel(
             )
 
         def raise_rows(h):
-            own = oa_slots[:, :, h * HALF : (h + 1) * HALF]
-            nc.vector.tensor_tensor(ha[:], za[h][:].rearrange("p t j -> p j t"), own.rearrange("p t j -> p j t"), MAX)
+            own = oa_slots[h][:]
+            nc.vector.tensor_tensor(ha[h], za[h][:].rearrange("p t j -> p j t"), own.rearrange("p t j -> p j t"), MAX)
 
         def quantize_rows(h):
             nc.vector.quantize_mx(
                 out=ha_words[h][:].bitcast(E5M2X4),
                 scales=ha_scales[h][:],
-                in_=ha[:].rearrange("p j t -> p (j t)"),
+                in_=ha[h].rearrange("p j t -> p (j t)"),
             )
 
         def meet(h):
@@ -173,21 +179,25 @@ def tile_list_meet_added_lagged_placed_kernel(
                 start=True,
                 stop=True,
             )
-            nc.scalar.activation(staged[h][:], scores[h][:], COPY, scale=GAIN)
 
         lag_columns(0)
-        raise_rows(0)
         lag_columns(1)
-        quantize_rows(0)
+        raise_rows(0)
+        hb_words = sb.tile([P, I], U32, name="hb_words", tag="reused", align_bytes=64)
         nc.vector.quantize_mx(
-            out=hb_words[:].bitcast(E5M2X4), scales=hb_scales[:], in_=shared[:, 0:512].bitcast(BF16)
+            out=hb_words[:].bitcast(E5M2X4), scales=hb_scales[:], in_=hb[:].rearrange("p i t -> p (i t)")
         )
+        quantize_rows(0)
         meet(0)
         raise_rows(1)
+        staged_first = sb.tile([P, I], F32, name="staged_first", tag="reused_second", align_bytes=64)
+        nc.scalar.activation(staged_first[:], scores[0][:], COPY, scale=GAIN)
         quantize_rows(1)
         meet(1)
-        nc.vector.tensor_copy(boards[0][:].indirect(list_q[:]), staged[0][:])
-        nc.scalar.activation(boards[1][:].indirect(list_q[:]), staged[1][:], COPY)
+        staged_second = sb.tile([P, I], F32, name="staged_second", align_bytes=64)
+        nc.scalar.activation(staged_second[:], scores[1][:], COPY, scale=GAIN)
+        nc.vector.tensor_copy(boards[0][:].indirect(list_q[:]), staged_first[:])
+        nc.scalar.activation(boards[1][:].indirect(list_q[:]), staged_second[:], COPY)
 
         pieces = [(h, lo, lo + 256) for h in range(2) for lo in range(0, Q, 256)]
         for n, (h, lo, hi) in enumerate(pieces):

@@ -20,16 +20,14 @@ COPY = mybir.ActivationFunctionType.Copy
 
 P = 128
 PACK = 4
+BLOCKS = 16
+ENTRIES = 16
 HALF = 128
 LAG = 0.6
 GAIN = 0.04
-
-
-def load_scale_plane(queue_low, queue_high, plane, scales):
-    rows = scales[0].bitcast(I32)
-    words = rows.shape[1]
-    queue_low.dma_start(out=plane[0:98, :].bitcast(I32), in_=rows[0:14, :].unsqueeze(0).to_broadcast([7, 14, words]))
-    queue_high.dma_start(out=plane[98:P, :].bitcast(I32), in_=rows[14:16, :].unsqueeze(0).to_broadcast([15, 2, words]))
+PIECE = 256
+ODD_SPLIT = 511
+EDGE = 16
 
 
 def load_scale_quadrant(queue, plane, scales, quad):
@@ -40,22 +38,29 @@ def load_scale_quadrant(queue, plane, scales, quad):
     )
 
 
-def deal_columns(copy, word, dealt, raw):
+def load_scale_plane(queue_low, queue_high, plane, scales):
+    rows = scales[0].bitcast(I32)
+    width = rows.shape[1]
+    queue_low.dma_start(out=plane[0:98, :].bitcast(I32), in_=rows[0:14, :].unsqueeze(0).to_broadcast([7, 14, width]))
+    queue_high.dma_start(out=plane[98:P, :].bitcast(I32), in_=rows[14:16, :].unsqueeze(0).to_broadcast([15, 2, width]))
+
+
+def deal_columns(copy, dealt, raw):
     copy(
-        out=dealt[:].bitcast(word).rearrange("p (t b w) -> p t b w", t=PACK, b=16),
-        in_=raw[:].bitcast(word).rearrange("p (b t w) -> p t b w", t=PACK, b=16),
+        out=dealt[:].bitcast(U32).rearrange("p (t b w) -> p t b w", t=PACK, b=BLOCKS),
+        in_=raw[:].bitcast(U32).rearrange("p (b t w) -> p t b w", t=PACK, b=BLOCKS),
     )
 
 
-def first_product(nc, bank, w_words, w_scales, x_words, x_scales, half):
+def first_product(nc, bank, w_words, w_scales, picked_words, picked_scales, half):
     cols = slice(half * HALF, (half + 1) * HALF)
     for t in range(PACK):
         nc.tensor.matmul_mx(
             out=bank[:, t, :],
             lhsT=w_words[:, 2 * P * t : 2 * P * (t + 1)].bitcast(E2M1X4),
             lhsT_scale=w_scales[:, P * t : P * (t + 1)],
-            rhs=x_words[:, cols].bitcast(E5M2X4),
-            rhs_scale=x_scales[:, cols],
+            rhs=picked_words[:, cols].bitcast(E5M2X4),
+            rhs_scale=picked_scales[:, cols],
             start=True,
             stop=True,
         )
@@ -70,9 +75,9 @@ def tile_list_meet_added_lagged_placed_kernel(
         sb = ctx.enter_context(tc.tile_pool(name="sb", bufs=1))
         psum = ctx.enter_context(tc.psum_pool(name="psum", bufs=1))
 
-        list_a = lists.tile([P, J // 16], U16, name="list_a")
-        list_b = lists.tile([P, I // 16], U16, name="list_b")
-        list_q = lists.tile([P, I // 16], U16, name="list_q")
+        list_a = lists.tile([P, J // ENTRIES], U16, name="list_a")
+        list_b = lists.tile([P, I // ENTRIES], U16, name="list_b")
+        list_q = lists.tile([P, I // ENTRIES], U16, name="list_q")
 
         x_words = sb.tile([P, T], U32, name="x_words", align_bytes=64)
         x_scales = sb.tile([P, T], U8, name="x_scales", align_bytes=64)
@@ -81,8 +86,8 @@ def tile_list_meet_added_lagged_placed_kernel(
         wa_scales_raw = sb.tile([P, R], U8, name="wa_scales_raw", align_bytes=64)
         wb_scales_raw = sb.tile([P, R], U8, name="wb_scales_raw", align_bytes=64)
         oa_first = sb.tile([P, PACK, HALF], F32, name="oa_first", tag="reused", align_bytes=64)
-        oa_second = sb.tile([P, PACK, HALF], F32, name="oa_second", tag="reused_second", align_bytes=64)
-        oa_slots = [oa_first, oa_second]
+        shared = sb.tile([P, I - EDGE + PACK * HALF], F32, name="shared", align_bytes=64)
+        oa_slots = [oa_first[:], shared[:, I - EDGE :].rearrange("p (t j) -> p t j", t=PACK)]
         old_rows = [sb.tile([P, Q], F32, name=f"old_rows{h}", align_bytes=64) for h in range(2)]
 
         nc.sync.dma_start(list_b[:], offs2)
@@ -105,8 +110,8 @@ def tile_list_meet_added_lagged_placed_kernel(
 
         boards = [sb.tile([P, Q], F32, name=f"board{h}", align_bytes=64) for h in range(2)]
         lagged = sb.tile([P, I, PACK], F32, name="lagged", align_bytes=64)
-        nc.vector.memset(boards[0][:, 0:511], 0.0)
-        nc.vector.memset(boards[0][:, 511:Q], 0.0)
+        nc.vector.memset(boards[0][:, 0:ODD_SPLIT], 0.0)
+        nc.vector.memset(boards[0][:, ODD_SPLIT:Q], 0.0)
         nc.vector.memset(boards[1][:], 0.0)
         nc.scalar.copy(out=lagged[:, 0, :], in_=boards[0][:, 0:PACK])
 
@@ -114,22 +119,22 @@ def tile_list_meet_added_lagged_placed_kernel(
         wb_dealt = sb.tile([P, 2 * R], U8, name="wb_dealt", align_bytes=64)
         wa_scales_dealt = sb.tile([P, R], U8, name="wa_scales_dealt", align_bytes=64)
         wb_scales_dealt = sb.tile([P, R], U8, name="wb_scales_dealt", align_bytes=64)
-        deal_columns(nc.scalar.copy, U32, wb_dealt, wb_raw)
+        deal_columns(nc.scalar.copy, wb_dealt, wb_raw)
 
         xb_words = sb.tile([P, I], U32, name="xb_words", align_bytes=64)
         xb_scales = sb.tile([P, I], U8, name="xb_scales", align_bytes=64)
         xa_words = sb.tile([P, J], U32, name="xa_words", align_bytes=64)
         xa_scales = sb.tile([P, J], U8, name="xa_scales", align_bytes=64)
-        for words, scales, picks in ((xb_words, xb_scales, list_b), (xa_words, xa_scales, list_a)):
+        for picked_words, picked_scales, picks in ((xb_words, xb_scales, list_b), (xa_words, xa_scales, list_a)):
             for h in range(2):
                 cols = slice(h * HALF, (h + 1) * HALF)
-                entries = picks[:, h * HALF // 16 : (h + 1) * HALF // 16]
-                nc.vector.tensor_copy(words[:, cols], x_words[:].indirect(entries))
-                nc.vector.tensor_copy(scales[:, cols], x_scales[:].indirect(entries))
+                entries = picks[:, h * HALF // ENTRIES : (h + 1) * HALF // ENTRIES]
+                nc.vector.tensor_copy(picked_words[:, cols], x_words[:].indirect(entries))
+                nc.vector.tensor_copy(picked_scales[:, cols], x_scales[:].indirect(entries))
 
-        deal_columns(nc.scalar.copy, U32, wb_scales_dealt, wb_scales_raw)
-        deal_columns(nc.gpsimd.tensor_copy, U32, wa_dealt, wa_raw)
-        deal_columns(nc.gpsimd.tensor_copy, U32, wa_scales_dealt, wa_scales_raw)
+        deal_columns(nc.scalar.copy, wb_scales_dealt, wb_scales_raw)
+        deal_columns(nc.gpsimd.tensor_copy, wa_dealt, wa_raw)
+        deal_columns(nc.gpsimd.tensor_copy, wa_scales_dealt, wa_scales_raw)
 
         zb = [psum.tile([P, PACK, HALF], F32, name=f"zb{h}") for h in range(2)]
         za = [psum.tile([P, PACK, HALF], F32, name=f"za{h}") for h in range(2)]
@@ -159,8 +164,9 @@ def tile_list_meet_added_lagged_placed_kernel(
             )
 
         def raise_rows(h):
-            own = oa_slots[h][:]
-            nc.vector.tensor_tensor(ha[h], za[h][:].rearrange("p t j -> p j t"), own.rearrange("p t j -> p j t"), MAX)
+            nc.vector.tensor_tensor(
+                ha[h], za[h][:].rearrange("p t j -> p j t"), oa_slots[h].rearrange("p t j -> p j t"), MAX
+            )
 
         def quantize_rows(h):
             nc.vector.quantize_mx(
@@ -169,7 +175,7 @@ def tile_list_meet_added_lagged_placed_kernel(
                 in_=ha[h].rearrange("p j t -> p (j t)"),
             )
 
-        def meet(h):
+        def meet(h, hb_words):
             nc.tensor.matmul_mx(
                 out=scores[h][:],
                 lhsT=ha_words[h][:].bitcast(E5M2X4),
@@ -188,18 +194,20 @@ def tile_list_meet_added_lagged_placed_kernel(
             out=hb_words[:].bitcast(E5M2X4), scales=hb_scales[:], in_=hb[:].rearrange("p i t -> p (i t)")
         )
         quantize_rows(0)
-        meet(0)
+        meet(0, hb_words)
+        staged_first = shared[:, 0:I]
+        nc.scalar.activation(staged_first[:, 0 : I - EDGE], scores[0][:, 0 : I - EDGE], COPY, scale=GAIN)
         raise_rows(1)
-        staged_first = sb.tile([P, I], F32, name="staged_first", tag="reused_second", align_bytes=64)
-        nc.scalar.activation(staged_first[:], scores[0][:], COPY, scale=GAIN)
+        nc.scalar.activation(staged_first[:, I - EDGE : I], scores[0][:, I - EDGE : I], COPY, scale=GAIN)
         quantize_rows(1)
-        meet(1)
+        meet(1, hb_words)
         staged_second = sb.tile([P, I], F32, name="staged_second", align_bytes=64)
         nc.scalar.activation(staged_second[:], scores[1][:], COPY, scale=GAIN)
-        nc.vector.tensor_copy(boards[0][:].indirect(list_q[:]), staged_first[:])
+
+        nc.vector.tensor_copy(boards[0][:].indirect(list_q[:]), staged_first)
         nc.scalar.activation(boards[1][:].indirect(list_q[:]), staged_second[:], COPY)
 
-        pieces = [(h, lo, lo + 256) for h in range(2) for lo in range(0, Q, 256)]
+        pieces = [(h, lo, lo + PIECE) for h in range(2) for lo in range(0, Q, PIECE)]
         for n, (h, lo, hi) in enumerate(pieces):
             result = sb.tile([P, hi - lo], F32, name=f"result{n}", align_bytes=64)
             nc.vector.scalar_tensor_tensor(

from contextlib import ExitStack

import concourse.mybir as mybir

K, T, J, I, R, Q = 512, 512, 256, 256, 512, 1024
FLOPS = 2 * K * R * J + 2 * K * R * I + 2 * R * J * I

F32 = mybir.dt.float32
BF16 = mybir.dt.bfloat16
I32 = mybir.dt.int32
U32 = mybir.dt.uint32
U16 = mybir.dt.uint16
U8 = mybir.dt.uint8
E5M2X4 = mybir.dt.float8_e5m2_x4
E2M1X4 = mybir.dt.float4_e2m1fn_x4
MULT = mybir.AluOpType.mult
ADD = mybir.AluOpType.add
MAX = mybir.AluOpType.max
COPY = mybir.ActivationFunctionType.Copy

P = 128
PACK = 4
BLOCKS = 16
ENTRIES = 16
HALF = 128
LAG = 0.6
GAIN = 0.04
PIECE = 256
ODD_SPLIT = 511
EDGE = 16


def load_scale_quadrant(queue, plane, scales, quad):
    rows = scales[0].bitcast(I32)[4 * quad : 4 * quad + 4, :]
    queue.dma_start(
        out=plane[32 * quad : 32 * quad + 32, :].bitcast(I32),
        in_=rows.unsqueeze(0).to_broadcast([8, 4, rows.shape[1]]),
    )


def load_scale_plane(queue_low, queue_high, plane, scales):
    rows = scales[0].bitcast(I32)
    width = rows.shape[1]
    queue_low.dma_start(out=plane[0:98, :].bitcast(I32), in_=rows[0:14, :].unsqueeze(0).to_broadcast([7, 14, width]))
    queue_high.dma_start(out=plane[98:P, :].bitcast(I32), in_=rows[14:16, :].unsqueeze(0).to_broadcast([15, 2, width]))


def deal_columns(copy, dealt, raw):
    copy(
        out=dealt[:].bitcast(U32).rearrange("p (t b w) -> p t b w", t=PACK, b=BLOCKS),
        in_=raw[:].bitcast(U32).rearrange("p (b t w) -> p t b w", t=PACK, b=BLOCKS),
    )


def first_product(nc, bank, w_words, w_scales, picked_words, picked_scales, half):
    cols = slice(half * HALF, (half + 1) * HALF)
    for t in range(PACK):
        nc.tensor.matmul_mx(
            out=bank[:, t, :],
            lhsT=w_words[:, 2 * P * t : 2 * P * (t + 1)].bitcast(E2M1X4),
            lhsT_scale=w_scales[:, P * t : P * (t + 1)],
            rhs=picked_words[:, cols].bitcast(E5M2X4),
            rhs_scale=picked_scales[:, cols],
            start=True,
            stop=True,
        )


def tile_list_meet_added_lagged_placed_kernel(
    tc, xt_words, xt_scales, wa_words, wa_scales, oa, wb_words, wb_scales, old, offs, offs2, offs3, out
):
    nc = tc.nc
    with ExitStack() as ctx:
        lists = ctx.enter_context(tc.tile_pool(name="lists", bufs=1))
        sb = ctx.enter_context(tc.tile_pool(name="sb", bufs=1))
        psum = ctx.enter_context(tc.psum_pool(name="psum", bufs=1))

        list_a = lists.tile([P, J // ENTRIES], U16, name="list_a")
        list_b = lists.tile([P, I // ENTRIES], U16, name="list_b")
        list_q = lists.tile([P, I // ENTRIES], U16, name="list_q")

        x_words = sb.tile([P, T], U32, name="x_words", align_bytes=64)
        x_scales = sb.tile([P, T], U8, name="x_scales", align_bytes=64)
        wa_raw = sb.tile([P, 2 * R], U8, name="wa_raw", align_bytes=64)
        wb_raw = sb.tile([P, 2 * R], U8, name="wb_raw", align_bytes=64)
        wa_scales_raw = sb.tile([P, R], U8, name="wa_scales_raw", align_bytes=64)
        wb_scales_raw = sb.tile([P, R], U8, name="wb_scales_raw", align_bytes=64)
        oa_first = sb.tile([P, PACK, HALF], F32, name="oa_first", tag="reused", align_bytes=64)
        shared = sb.tile([P, I - EDGE + PACK * HALF], F32, name="shared", align_bytes=64)
        oa_slots = [oa_first[:], shared[:, I - EDGE :].rearrange("p (t j) -> p t j", t=PACK)]
        old_rows = [sb.tile([P, Q], F32, name=f"old_rows{h}", align_bytes=64) for h in range(2)]

        nc.sync.dma_start(list_b[:], offs2)
        nc.sync.dma_start(out=x_words[:].bitcast(I32), in_=xt_words[0].rearrange("p c r -> p (c r)").bitcast(I32))
        for quad in range(4):
            load_scale_quadrant(nc.sync, x_scales, xt_scales, quad)
        nc.sync.dma_start(out=wb_raw[:].bitcast(I32), in_=wb_words[0].bitcast(I32))
        load_scale_plane(nc.scalar, nc.gpsimd, wb_scales_raw, wb_scales)
        nc.gpsimd.dma_start(out=wa_raw[:].bitcast(I32), in_=wa_words[0].bitcast(I32))
        nc.sync.dma_start(list_a[:], offs)
        for quad in range(4):
            load_scale_quadrant(nc.sync, wa_scales_raw, wa_scales, quad)
        oa_by_slot = oa.rearrange("(b t u) j -> t b u j", t=PACK, u=8)
        for h in range(2):
            for t in range(PACK):
                nc.sync.dma_start(out=oa_slots[h][:, t, :], in_=oa_by_slot[t][:, :, h * HALF : (h + 1) * HALF])
        nc.sync.dma_start(list_q[:], offs3)
        for h in range(2):
            nc.sync.dma_start(out=old_rows[h][:], in_=old[h * P : (h + 1) * P, :])

        boards = [sb.tile([P, Q], F32, name=f"board{h}", align_bytes=64) for h in range(2)]
        lagged = sb.tile([P, I, PACK], F32, name="lagged", align_bytes=64)
        nc.vector.memset(boards[0][:, 0:ODD_SPLIT], 0.0)
        nc.vector.memset(boards[0][:, ODD_SPLIT:Q], 0.0)
        nc.vector.memset(boards[1][:], 0.0)
        nc.scalar.copy(out=lagged[:, 0, :], in_=boards[0][:, 0:PACK])

        wa_dealt = sb.tile([P, 2 * R], U8, name="wa_dealt", align_bytes=64)
        wb_dealt = sb.tile([P, 2 * R], U8, name="wb_dealt", align_bytes=64)
        wa_scales_dealt = sb.tile([P, R], U8, name="wa_scales_dealt", align_bytes=64)
        wb_scales_dealt = sb.tile([P, R], U8, name="wb_scales_dealt", align_bytes=64)
        deal_columns(nc.scalar.copy, wb_dealt, wb_raw)

        xb_words = sb.tile([P, I], U32, name="xb_words", align_bytes=64)
        xb_scales = sb.tile([P, I], U8, name="xb_scales", align_bytes=64)
        xa_words = sb.tile([P, J], U32, name="xa_words", align_bytes=64)
        xa_scales = sb.tile([P, J], U8, name="xa_scales", align_bytes=64)
        for picked_words, picked_scales, picks in ((xb_words, xb_scales, list_b), (xa_words, xa_scales, list_a)):
            for h in range(2):
                cols = slice(h * HALF, (h + 1) * HALF)
                entries = picks[:, h * HALF // ENTRIES : (h + 1) * HALF // ENTRIES]
                nc.vector.tensor_copy(picked_words[:, cols], x_words[:].indirect(entries))
                nc.vector.tensor_copy(picked_scales[:, cols], x_scales[:].indirect(entries))

        deal_columns(nc.scalar.copy, wb_scales_dealt, wb_scales_raw)
        deal_columns(nc.gpsimd.tensor_copy, wa_dealt, wa_raw)
        deal_columns(nc.gpsimd.tensor_copy, wa_scales_dealt, wa_scales_raw)

        zb = [psum.tile([P, PACK, HALF], F32, name=f"zb{h}") for h in range(2)]
        za = [psum.tile([P, PACK, HALF], F32, name=f"za{h}") for h in range(2)]
        scores = [psum.tile([P, I], F32, name=f"scores{h}") for h in range(2)]

        for h in range(2):
            first_product(nc, zb[h], wb_dealt, wb_scales_dealt, xb_words, xb_scales, h)
            width = min(HALF, I - 1 - h * HALF)
            nc.scalar.copy(
                out=lagged[:, h * HALF + 1 : h * HALF + 1 + width, :],
                in_=zb[h][:, :, 0:width].rearrange("p t i -> p i t"),
            )
        for h in range(2):
            first_product(nc, za[h], wa_dealt, wa_scales_dealt, xa_words, xa_scales, h)

        hb = sb.tile([P, I, PACK], BF16, name="hb", align_bytes=64)
        ha_first = sb.tile([P, HALF, PACK], BF16, name="ha_first", align_bytes=64)
        ha = [ha_first[:], hb[:, 0:HALF, :]]
        hb_scales = sb.tile([P, I], U8, name="hb_scales", align_bytes=64)
        ha_words = [sb.tile([P, HALF], U32, name=f"ha_words{h}", align_bytes=64) for h in range(2)]
        ha_scales = [sb.tile([P, HALF], U8, name=f"ha_scales{h}", align_bytes=64) for h in range(2)]

        def lag_columns(h):
            cols = slice(h * HALF, (h + 1) * HALF)
            nc.vector.scalar_tensor_tensor(
                hb[:, cols, :], lagged[:, cols, :], -LAG, zb[h][:].rearrange("p t i -> p i t"), MULT, ADD
            )

        def raise_rows(h):
            nc.vector.tensor_tensor(
                ha[h], za[h][:].rearrange("p t j -> p j t"), oa_slots[h].rearrange("p t j -> p j t"), MAX
            )

        def quantize_rows(h):
            nc.vector.quantize_mx(
                out=ha_words[h][:].bitcast(E5M2X4),
                scales=ha_scales[h][:],
                in_=ha[h].rearrange("p j t -> p (j t)"),
            )

        def meet(h, hb_words):
            nc.tensor.matmul_mx(
                out=scores[h][:],
                lhsT=ha_words[h][:].bitcast(E5M2X4),
                lhsT_scale=ha_scales[h][:],
                rhs=hb_words[:].bitcast(E5M2X4),
                rhs_scale=hb_scales[:],
                start=True,
                stop=True,
            )

        lag_columns(0)
        lag_columns(1)
        raise_rows(0)
        hb_words = sb.tile([P, I], U32, name="hb_words", tag="reused", align_bytes=64)
        nc.vector.quantize_mx(
            out=hb_words[:].bitcast(E5M2X4), scales=hb_scales[:], in_=hb[:].rearrange("p i t -> p (i t)")
        )
        quantize_rows(0)
        meet(0, hb_words)
        staged_first = shared[:, 0:I]
        nc.scalar.activation(staged_first[:, 0 : I - EDGE], scores[0][:, 0 : I - EDGE], COPY, scale=GAIN)
        raise_rows(1)
        nc.scalar.activation(staged_first[:, I - EDGE : I], scores[0][:, I - EDGE : I], COPY, scale=GAIN)
        quantize_rows(1)
        meet(1, hb_words)
        staged_second = sb.tile([P, I], F32, name="staged_second", align_bytes=64)
        nc.scalar.activation(staged_second[:], scores[1][:], COPY, scale=GAIN)

        nc.vector.tensor_copy(boards[0][:].indirect(list_q[:]), staged_first)
        nc.scalar.activation(boards[1][:].indirect(list_q[:]), staged_second[:], COPY)

        pieces = [(h, lo, lo + PIECE) for h in range(2) for lo in range(0, Q, PIECE)]
        for n, (h, lo, hi) in enumerate(pieces):
            result = sb.tile([P, hi - lo], F32, name=f"result{n}", align_bytes=64)
            nc.vector.scalar_tensor_tensor(
                result[:], old_rows[h][:, lo:hi], -GAIN, boards[h][:, lo:hi], MULT, ADD
            )
            nc.sync.dma_start(out=out[h * P : (h + 1) * P, lo:hi], in_=result[:])
